import numpy as np
import ml_dtypes


def mxq(x, axis, fmt="e4m3"):
    dtype, down = {"e4m3": (ml_dtypes.float8_e4m3fn, 7), "e5m2": (ml_dtypes.float8_e5m2, 14)}[fmt]
    v = np.moveaxis(np.asarray(x, np.float32).astype(ml_dtypes.bfloat16).astype(np.float64), axis, -1)
    blocks = v.reshape(v.shape[:-1] + (-1, 32))
    amax = np.abs(blocks).max(-1, keepdims=True)
    byte = np.maximum(np.where(amax > 0, np.frexp(amax)[1] - 1 + 127, 0) - down, 1)
    scale = np.exp2(byte - 127.0)
    codes = (blocks / scale).astype(np.float32).astype(dtype).astype(np.float64)
    return np.moveaxis((codes * scale).reshape(v.shape), -1, axis)


WIDE = False


def mx_kscale(k):
    if not WIDE:
        return np.ones(k)
    levels = np.array([10, -10, 5, -5, 0])
    if k % 512:
        return np.exp2(np.random.permutation(np.resize(levels, k // 32))).repeat(32)
    a = np.empty((k // 512, 16))
    for p in range(k // 512):
        a[p, :8] = np.random.permutation(np.resize(levels, 8))
        for g in range(8):
            far = levels[np.abs(levels - a[p, g]) >= 10]
            a[p, g + 8] = far[np.random.randint(len(far))]
    return np.exp2(a.ravel()).repeat(32)


def f64(x):
    return np.asarray(x).astype(np.float64)


def striped(idx):
    return np.tile(idx.reshape(-1, 16).T, (8, 1)).astype(np.uint16)


def unstriped(offs):
    return offs[:16].T.reshape(-1).astype(np.int64)


def pack_weight(w):
    k, n = w.shape
    w = f64(np.asarray(w, np.float32).astype(ml_dtypes.bfloat16)).reshape(k // 32, 32, n)
    amax = np.abs(w).max(1)
    byte = np.clip(np.where(amax > 0, np.frexp(amax)[1] - 1 + 127 - 7, 1), 1, 254)
    scaled = (w * np.exp2(127.0 - byte)[:, None, :]).reshape(k, n).astype(np.float32)
    words = np.ascontiguousarray(scaled.reshape(k // 512, 128, 4, n).transpose(0, 1, 3, 2)).astype(ml_dtypes.float8_e4m3fn).view(np.uint8)
    return words, np.ascontiguousarray(byte.astype(np.uint8).reshape(k // 512, 16, n))


def unpack_weight(words, scales):
    g, p, n, _ = words.shape
    vals = np.ascontiguousarray(words).view(ml_dtypes.float8_e4m3fn).astype(np.float64) * np.repeat(np.exp2(scales.astype(np.float64) - 127.0), 8, axis=1)[..., None]
    return vals.transpose(0, 1, 3, 2).reshape(g * 512, n)


K, T, S, N, U = 1024, 2048, 512, 256, 256
P = 2 ** 7


def setup_inputs():
    n = np.random.standard_normal
    s = mx_kscale(K)[:, None]
    packed_xT = pack_weight(n((K, T)) * s)
    return {
        "x_words": packed_xT[0],
        "x_scales": packed_xT[1],
        "w1": (n((K, N)) / np.sqrt(K) / s).astype(np.float32),
        "pose": (n((N, U))).astype(np.float32),
        "info": (np.tile(np.random.uniform(0.4, 1.4, S), (P, 1))).astype(np.float32),
        "mu": (np.tile(np.random.uniform(0.5, 2.0, S), (P, 1))).astype(np.float32),
        "offs": striped(np.random.permutation(T)[:S]),
        "ia": striped(np.random.permutation(np.concatenate([np.arange(U), np.random.randint(0, U, S - U)]))),
        "ib": striped(np.random.permutation(np.concatenate([np.arange(U), np.random.randint(0, U, S - U)]))),
    }


def reference(x_words, x_scales, w1, pose, info, mu, offs, ia, ib):
    xq = unpack_weight(x_words, x_scales)[:, unstriped(offs)]
    y = mxq(f64(w1), 0, "e4m3").T @ xq
    res = f64(pose)[:, unstriped(ib)] - f64(pose)[:, unstriped(ia)] - y
    sw = f64(mu)[:1] / (f64(mu)[:1] + f64(info)[:1] * ((res) ** 2))
    return f64(info)[:1] * ((sw * res) ** 2) + f64(mu)[:1] * ((-1.0 * sw + 1.0) ** 2)

@@ -1,0 +1,144 @@
+from contextlib import ExitStack
+
+import concourse.mybir as mybir
+from concourse.masks import make_identity
+
+K, T, S, N, U = 1024, 2048, 512, 256, 256
+FLOPS = 2 * K * S * N
+
+F32 = mybir.dt.float32
+BF16 = mybir.dt.bfloat16
+I32 = mybir.dt.int32
+U32 = mybir.dt.uint32
+U16 = mybir.dt.uint16
+U8 = mybir.dt.uint8
+FP8X4 = mybir.dt.float8_e4m3fn_x4
+ACT = mybir.ActivationFunctionType
+ALU = mybir.AluOpType
+
+P = 128
+PACK = 4
+PASSES = K // (P * PACK)
+BLOCKS = N // P
+TILES = S // P
+WINDOW = 704
+SPARE = WINDOW - U
+
+
+def tile_picked_yposgr_cost_p_kernel(tc, x_words, x_scales, w1, pose, info, mu, offs, ia, ib, out):
+    nc = tc.nc
+    with ExitStack() as ctx:
+        keep = ctx.enter_context(tc.tile_pool(name="keep", bufs=1))
+        ybanks = ctx.enter_context(tc.psum_pool(name="ybanks", bufs=1))
+        turns = ctx.enter_context(tc.psum_pool(name="turns", bufs=2))
+
+        ib_sb = keep.tile([P, S // 16], U16, name="ib_sb")
+        ia_sb = keep.tile([P, S // 16], U16, name="ia_sb")
+        offs_sb = keep.tile([P, S // 16], U16, name="offs_sb")
+        pose_sb = keep.tile([P, BLOCKS * U + SPARE], F32, name="pose_sb")
+        neg_pose = keep.tile([P, BLOCKS * U + SPARE], F32, name="neg_pose")
+        scale_table = keep.tile([P, T], U8, name="scale_table", align_bytes=64)
+        word_table = [keep.tile([P, T], I32, name=f"word_table{g}", align_bytes=64) for g in range(PASSES)]
+        w_raw = keep.tile([P, PASSES, PACK, N], F32, name="w_raw")
+        edge_rows = keep.tile([P, P], F32, name="edge_rows")
+        ident = keep.tile([P, P], F32, name="ident")
+        warm = keep.tile([P, 2], F32, name="warm")
+
+        nc.gpsimd.memset(scale_table[:].bitcast(I32), 0)
+        nc.vector.memset(warm[:, 0:1], 1.0)
+        nc.vector.memset(pose_sb[:, BLOCKS * U :], 0.0)
+        nc.vector.memset(neg_pose[:, BLOCKS * U :], 0.0)
+        nc.vector.memset(edge_rows[: P - 2 * TILES, :], 0.0)
+
+        nc.sync.dma_start(ib_sb[:], ib)
+        nc.sync.dma_start(pose_sb[:, : BLOCKS * U].rearrange("p (b u) -> p b u", b=BLOCKS), pose.rearrange("(b p) u -> p b u", p=P))
+        nc.sync.dma_start(ia_sb[:], ia)
+        nc.sync.dma_start(w_raw[:].rearrange("p g j n -> p g (j n)"), w1.rearrange("(g p j) n -> p g (j n)", p=P, j=PACK))
+        for q in range(4):
+            nc.sync.dma_start(scale_table[32 * q : 32 * q + 4 * PASSES, :].bitcast(I32), x_scales[:, 4 * q : 4 * q + 4, :].bitcast(I32))
+        nc.sync.dma_start(offs_sb[:], offs)
+        for g in range(PASSES):
+            nc.sync.dma_start(word_table[g][:], x_words[g].rearrange("p n t -> p (n t)").bitcast(I32))
+        nc.scalar.activation(warm[:, 1:2], warm[:, 0:1], ACT.Abs_reciprocal_sqrt)
+        nc.gpsimd.dma_start(edge_rows[P - 2 * TILES : P - TILES, :], info[0].rearrange("(t c) -> t c", c=P))
+        nc.gpsimd.dma_start(edge_rows[P - TILES :, :], mu[0].rearrange("(t c) -> t c", c=P))
+        make_identity(nc, ident[:])
+
+        nc.scalar.activation(neg_pose[:, : BLOCKS * U], pose_sb[:, : BLOCKS * U], ACT.Copy, scale=-1.0)
+
+        ends = {}
+        for b in range(BLOCKS):
+            for name, table, offsets in (("b", pose_sb, ib_sb), ("a", neg_pose, ia_sb)):
+                picked = keep.tile([P, S], F32, name=f"end_{name}{b}")
+                nc.vector.tensor_copy(picked[:], table[:, b * U : b * U + WINDOW].indirect(offsets[:]))
+                ends[name, b] = picked
+
+        w_bf = keep.tile([P, PASSES, N, PACK], BF16, name="w_bf", align_bytes=64)
+        for g in range(PASSES):
+            nc.scalar.copy(w_bf[:, g], w_raw[:, g].rearrange("p j n -> p n j"))
+        w_codes = keep.tile([P, PASSES * N], U32, name="w_codes", align_bytes=64)
+        w_scales = keep.tile([P, PASSES * N], U8, name="w_scales", align_bytes=64)
+        nc.vector.quantize_mx(out=w_codes[:].bitcast(FP8X4), scales=w_scales[:], in_=w_bf[:].rearrange("p g n j -> p (g n j)"))
+
+        diff_ps = [turns.tile([P, 2, N], F32, name=f"diff_ps{h}", tag="turn") for h in range(2)]
+        for b in range(BLOCKS):
+            for t in range(TILES):
+                target = diff_ps[t // 2][:, t % 2, b * P : (b + 1) * P]
+                nc.tensor.matmul(target, ends["b", b][:, t * P : (t + 1) * P], ident[:], start=True, stop=False, is_transpose=True)
+                nc.tensor.matmul(target, ends["a", b][:, t * P : (t + 1) * P], ident[:], start=False, stop=True, is_transpose=True)
+        diff = keep.tile([P, TILES, N], F32, name="diff")
+        for h in range(2):
+            nc.scalar.copy(diff[:, 2 * h : 2 * h + 2, :], diff_ps[h][:])
+
+        edge_cols = turns.tile([P, P], F32, name="edge_cols", tag="turn")
+        nc.tensor.transpose(edge_cols[:], edge_rows[:], ident[:])
+        recips = keep.tile([P, 2 * TILES], F32, name="recips")
+        inv_roots = keep.tile([P, 2 * TILES], F32, name="inv_roots")
+        nc.scalar.activation(inv_roots[:], edge_cols[:, P - 2 * TILES :], ACT.Abs_reciprocal_sqrt)
+        nc.scalar.activation(recips[:], inv_roots[:], ACT.Square)
+
+        x_scale = keep.tile([P, S], U8, name="x_scale", align_bytes=64)
+        nc.vector.tensor_copy(x_scale[:], scale_table[:].indirect(offs_sb[:]))
+        x_codes = [keep.tile([P, S], U32, name=f"x_codes{g}", align_bytes=64) for g in range(PASSES)]
+        nc.vector.tensor_copy(x_codes[0][:], word_table[0][:].bitcast(U32).indirect(offs_sb[:]))
+        y_ps = [ybanks.tile([P, N], F32, name=f"y_ps{t}") for t in range(TILES)]
+
+        def product(t, g):
+            cols = slice(t * P, (t + 1) * P)
+            nc.tensor.matmul_mx(
+                out=y_ps[t][:],
+                lhsT=x_codes[g][:, cols].bitcast(FP8X4),
+                lhsT_scale=x_scale[4 * g :, cols],
+                rhs=w_codes[:, g * N : (g + 1) * N].bitcast(FP8X4),
+                rhs_scale=w_scales[:, g * N : (g + 1) * N],
+                start=(g == 0),
+                stop=(g == PASSES - 1),
+            )
+
+        for t in range(TILES):
+            product(t, 0)
+        for h in range(2):
+            nc.vector.tensor_copy(x_codes[1][:, h * 256 : (h + 1) * 256], word_table[1][:].bitcast(U32).indirect(offs_sb[:, h * 16 : (h + 1) * 16]))
+            product(2 * h, 1)
+            product(2 * h + 1, 1)
+
+        res = [keep.tile([P, N], F32, name=f"res{t}") for t in range(TILES)]
+        sq = [keep.tile([P, N], F32, name=f"sq{t}") for t in range(TILES)]
+        damp = [keep.tile([P, N], F32, name=f"damp{t}") for t in range(TILES)]
+        root = [keep.tile([P, N], F32, name=f"root{t}") for t in range(TILES)]
+        cost = [keep.tile([P, BLOCKS, P], F32, name=f"cost{t}") for t in range(TILES)]
+        out_rows = out.rearrange("(b p) s -> p b s", p=P)
+        for t in range(TILES):
+            nc.vector.tensor_tensor(res[t][:], y_ps[t][:], diff[:, t, :], ALU.subtract)
+            if t == 3:
+                nc.vector.tensor_tensor(sq[t][:], res[t][:], res[t][:], ALU.mult)
+            else:
+                nc.scalar.activation(sq[t][:], res[t][:], ACT.Square)
+            nc.scalar.activation(damp[t][:], sq[t][:], ACT.Abs_reciprocal_sqrt, bias=recips[:, t : t + 1], scale=recips[:, TILES + t : TILES + t + 1])
+        for t in range(TILES):
+            nc.vector.tensor_tensor(root[t][:], res[t][:], damp[t][:], ALU.mult)
+            back = turns.tile([P, BLOCKS, P], F32, name=f"back{t}", tag="back" if t < 2 else "turn")
+            for b in range(BLOCKS):
+                nc.tensor.transpose(back[:, b, :], root[t][:, b * P : (b + 1) * P], ident[:])
+            nc.scalar.activation(cost[t][:], back[:], ACT.Square)
+            nc.sync.dma_start(out_rows[:, :, t * P : (t + 1) * P], cost[t][:])

@@ -35,8 +35,8 @@ def tile_picked_yposgr_cost_p_kernel(tc, x_words, x_scales, w1, pose, info, mu, 
         ib_sb = keep.tile([P, S // 16], U16, name="ib_sb")
         ia_sb = keep.tile([P, S // 16], U16, name="ia_sb")
         offs_sb = keep.tile([P, S // 16], U16, name="offs_sb")
-        pose_sb = keep.tile([P, BLOCKS * U + SPARE], F32, name="pose_sb")
-        neg_pose = keep.tile([P, BLOCKS * U + SPARE], F32, name="neg_pose")
+        poses = keep.tile([P, 2 * BLOCKS * U + SPARE], F32, name="poses")
+        start = {("a", 1): 0, ("a", 0): U, ("b", 1): 2 * U, ("b", 0): 3 * U}
         scale_table = keep.tile([P, T], U8, name="scale_table", align_bytes=64)
         word_table = [keep.tile([P, T], I32, name=f"word_table{g}", align_bytes=64) for g in range(PASSES)]
         w_raw = keep.tile([P, PASSES, PACK, N], F32, name="w_raw")
@@ -46,13 +46,13 @@ def tile_picked_yposgr_cost_p_kernel(tc, x_words, x_scales, w1, pose, info, mu, 
 
         nc.gpsimd.memset(scale_table[:].bitcast(I32), 0)
         nc.vector.memset(warm[:, 0:1], 1.0)
-        nc.vector.memset(pose_sb[:, BLOCKS * U :], 0.0)
-        nc.vector.memset(neg_pose[:, BLOCKS * U :], 0.0)
+        nc.vector.memset(poses[:, 2 * BLOCKS * U :], 0.0)
         nc.vector.memset(edge_rows[: P - 2 * TILES, :], 0.0)
 
         nc.sync.dma_start(ib_sb[:], ib)
-        nc.sync.dma_start(pose_sb[:, : BLOCKS * U].rearrange("p (b u) -> p b u", b=BLOCKS), pose.rearrange("(b p) u -> p b u", p=P))
+        nc.sync.dma_start(poses[:, 3 * U : 4 * U], pose[:P, :])
         nc.sync.dma_start(ia_sb[:], ia)
+        nc.sync.dma_start(poses[:, 2 * U : 3 * U], pose[P:, :])
         nc.sync.dma_start(w_raw[:].rearrange("p g j n -> p g (j n)"), w1.rearrange("(g p j) n -> p g (j n)", p=P, j=PACK))
         for q in range(4):
             nc.sync.dma_start(scale_table[32 * q : 32 * q + 4 * PASSES, :].bitcast(I32), x_scales[:, 4 * q : 4 * q + 4, :].bitcast(I32))
@@ -60,17 +60,18 @@ def tile_picked_yposgr_cost_p_kernel(tc, x_words, x_scales, w1, pose, info, mu, 
         for g in range(PASSES):
             nc.sync.dma_start(word_table[g][:], x_words[g].rearrange("p n t -> p (n t)").bitcast(I32))
         nc.scalar.activation(warm[:, 1:2], warm[:, 0:1], ACT.Abs_reciprocal_sqrt)
-        nc.gpsimd.dma_start(edge_rows[P - 2 * TILES : P - TILES, :], info[0].rearrange("(t c) -> t c", c=P))
-        nc.gpsimd.dma_start(edge_rows[P - TILES :, :], mu[0].rearrange("(t c) -> t c", c=P))
+        nc.scalar.dma_start(edge_rows[P - 2 * TILES : P - TILES, :], info[0].rearrange("(t c) -> t c", c=P))
+        nc.scalar.dma_start(edge_rows[P - TILES :, :], mu[0].rearrange("(t c) -> t c", c=P))
         make_identity(nc, ident[:])
 
-        nc.scalar.activation(neg_pose[:, : BLOCKS * U], pose_sb[:, : BLOCKS * U], ACT.Copy, scale=-1.0)
+        for b in range(BLOCKS):
+            nc.scalar.activation(poses[:, start["a", b] : start["a", b] + U], poses[:, start["b", b] : start["b", b] + U], ACT.Copy, scale=-1.0)
 
         ends = {}
         for b in range(BLOCKS):
-            for name, table, offsets in (("b", pose_sb, ib_sb), ("a", neg_pose, ia_sb)):
+            for name, offsets in (("b", ib_sb), ("a", ia_sb)):
                 picked = keep.tile([P, S], F32, name=f"end_{name}{b}")
-                nc.vector.tensor_copy(picked[:], table[:, b * U : b * U + WINDOW].indirect(offsets[:]))
+                nc.vector.tensor_copy(picked[:], poses[:, start[name, b] : start[name, b] + WINDOW].indirect(offsets[:]))
                 ends[name, b] = picked
 
         w_bf = keep.tile([P, PASSES, N, PACK], BF16, name="w_bf", align_bytes=64)

@@ -41,31 +41,37 @@ def tile_picked_yposgr_cost_p_kernel(tc, x_words, x_scales, w1, pose, info, mu, 
         word_table = [keep.tile([P, T], I32, name=f"word_table{g}", align_bytes=64) for g in range(PASSES)]
         w_raw = keep.tile([P, PASSES, PACK, N], F32, name="w_raw")
         edge_rows = keep.tile([P, P], F32, name="edge_rows")
+        inv_rows = keep.tile([P, P], F32, name="inv_rows")
         ident = keep.tile([P, P], F32, name="ident")
-        warm = keep.tile([P, 2], F32, name="warm")
 
         nc.gpsimd.memset(scale_table[:].bitcast(I32), 0)
-        nc.vector.memset(warm[:, 0:1], 1.0)
         nc.vector.memset(poses[:, 2 * BLOCKS * U :], 0.0)
-        nc.vector.memset(edge_rows[: P - 2 * TILES, :], 0.0)
+        nc.vector.memset(inv_rows[:], 0.0)
 
         nc.sync.dma_start(ib_sb[:], ib)
         nc.sync.dma_start(poses[:, 3 * U : 4 * U], pose[:P, :])
         nc.sync.dma_start(ia_sb[:], ia)
         nc.sync.dma_start(poses[:, 2 * U : 3 * U], pose[P:, :])
         nc.sync.dma_start(w_raw[:].rearrange("p g j n -> p g (j n)"), w1.rearrange("(g p j) n -> p g (j n)", p=P, j=PACK))
+        nc.sync.dma_start(offs_sb[:], offs)
+        nc.sync.dma_start(word_table[0][:], x_words[0].rearrange("p n t -> p (n t)").bitcast(I32))
         for q in range(4):
             nc.sync.dma_start(scale_table[32 * q : 32 * q + 4 * PASSES, :].bitcast(I32), x_scales[:, 4 * q : 4 * q + 4, :].bitcast(I32))
-        nc.sync.dma_start(offs_sb[:], offs)
-        for g in range(PASSES):
-            nc.sync.dma_start(word_table[g][:], x_words[g].rearrange("p n t -> p (n t)").bitcast(I32))
-        nc.scalar.activation(warm[:, 1:2], warm[:, 0:1], ACT.Abs_reciprocal_sqrt)
-        nc.scalar.dma_start(edge_rows[P - 2 * TILES : P - TILES, :], info[0].rearrange("(t c) -> t c", c=P))
-        nc.scalar.dma_start(edge_rows[P - TILES :, :], mu[0].rearrange("(t c) -> t c", c=P))
+        nc.sync.dma_start(word_table[1][:], x_words[1].rearrange("p n t -> p (n t)").bitcast(I32))
+        nc.scalar.dma_start(edge_rows[:TILES, :], info[0].rearrange("(t c) -> t c", c=P))
+        nc.scalar.dma_start(edge_rows[32 : 32 + TILES, :], mu[0].rearrange("(t c) -> t c", c=P))
+        nc.scalar.activation(inv_rows[:TILES, :], edge_rows[:TILES, :], ACT.Abs_reciprocal_sqrt)
         make_identity(nc, ident[:])
 
         for b in range(BLOCKS):
             nc.scalar.activation(poses[:, start["a", b] : start["a", b] + U], poses[:, start["b", b] : start["b", b] + U], ACT.Copy, scale=-1.0)
+
+        nc.scalar.activation(inv_rows[32 : 32 + TILES, :], edge_rows[32 : 32 + TILES, :], ACT.Abs_reciprocal_sqrt)
+        nc.scalar.activation(inv_rows[: 32 + TILES, :], inv_rows[: 32 + TILES, :], ACT.Square)
+        edge_cols = turns.tile([P, P], F32, name="edge_cols", tag="turn")
+        nc.tensor.transpose(edge_cols[:], inv_rows[:], ident[:])
+        recips = keep.tile([P, 32 + TILES], F32, name="recips")
+        nc.scalar.copy(recips[:], edge_cols[:, : 32 + TILES])
 
         ends = {}
         for b in range(BLOCKS):
@@ -79,7 +85,8 @@ def tile_picked_yposgr_cost_p_kernel(tc, x_words, x_scales, w1, pose, info, mu, 
             nc.scalar.copy(w_bf[:, g], w_raw[:, g].rearrange("p j n -> p n j"))
         w_codes = keep.tile([P, PASSES * N], U32, name="w_codes", align_bytes=64)
         w_scales = keep.tile([P, PASSES * N], U8, name="w_scales", align_bytes=64)
-        nc.vector.quantize_mx(out=w_codes[:].bitcast(FP8X4), scales=w_scales[:], in_=w_bf[:].rearrange("p g n j -> p (g n j)"))
+        for g in range(PASSES):
+            nc.vector.quantize_mx(out=w_codes[:, g * N : (g + 1) * N].bitcast(FP8X4), scales=w_scales[:, g * N : (g + 1) * N], in_=w_bf[:, g].rearrange("p n j -> p (n j)"))
 
         diff_ps = [turns.tile([P, 2, N], F32, name=f"diff_ps{h}", tag="turn") for h in range(2)]
         for b in range(BLOCKS):
@@ -91,15 +98,9 @@ def tile_picked_yposgr_cost_p_kernel(tc, x_words, x_scales, w1, pose, info, mu, 
         for h in range(2):
             nc.scalar.copy(diff[:, 2 * h : 2 * h + 2, :], diff_ps[h][:])
 
-        edge_cols = turns.tile([P, P], F32, name="edge_cols", tag="turn")
-        nc.tensor.transpose(edge_cols[:], edge_rows[:], ident[:])
-        recips = keep.tile([P, 2 * TILES], F32, name="recips")
-        inv_roots = keep.tile([P, 2 * TILES], F32, name="inv_roots")
-        nc.scalar.activation(inv_roots[:], edge_cols[:, P - 2 * TILES :], ACT.Abs_reciprocal_sqrt)
-        nc.scalar.activation(recips[:], inv_roots[:], ACT.Square)
-
         x_scale = keep.tile([P, S], U8, name="x_scale", align_bytes=64)
-        nc.vector.tensor_copy(x_scale[:], scale_table[:].indirect(offs_sb[:]))
+        for h in range(2):
+            nc.vector.tensor_copy(x_scale[:, h * 256 : (h + 1) * 256], scale_table[:].indirect(offs_sb[:, h * 16 : (h + 1) * 16]))
         x_codes = [keep.tile([P, S], U32, name=f"x_codes{g}", align_bytes=64) for g in range(PASSES)]
         nc.vector.tensor_copy(x_codes[0][:], word_table[0][:].bitcast(U32).indirect(offs_sb[:]))
         y_ps = [ybanks.tile([P, N], F32, name=f"y_ps{t}") for t in range(TILES)]
@@ -129,17 +130,46 @@ def tile_picked_yposgr_cost_p_kernel(tc, x_words, x_scales, w1, pose, info, mu, 
         root = [keep.tile([P, N], F32, name=f"root{t}") for t in range(TILES)]
         cost = [keep.tile([P, BLOCKS, P], F32, name=f"cost{t}") for t in range(TILES)]
         out_rows = out.rearrange("(b p) s -> p b s", p=P)
-        for t in range(TILES):
+
+        def residual(t):
             nc.vector.tensor_tensor(res[t][:], y_ps[t][:], diff[:, t, :], ALU.subtract)
-            if t == 3:
+
+        def damping(t, on_vector):
+            if on_vector:
                 nc.vector.tensor_tensor(sq[t][:], res[t][:], res[t][:], ALU.mult)
             else:
                 nc.scalar.activation(sq[t][:], res[t][:], ACT.Square)
-            nc.scalar.activation(damp[t][:], sq[t][:], ACT.Abs_reciprocal_sqrt, bias=recips[:, t : t + 1], scale=recips[:, TILES + t : TILES + t + 1])
-        for t in range(TILES):
-            nc.vector.tensor_tensor(root[t][:], res[t][:], damp[t][:], ALU.mult)
-            back = turns.tile([P, BLOCKS, P], F32, name=f"back{t}", tag="back" if t < 2 else "turn")
-            for b in range(BLOCKS):
-                nc.tensor.transpose(back[:, b, :], root[t][:, b * P : (b + 1) * P], ident[:])
-            nc.scalar.activation(cost[t][:], back[:], ACT.Square)
-            nc.sync.dma_start(out_rows[:, :, t * P : (t + 1) * P], cost[t][:])
+            nc.scalar.activation(damp[t][:], sq[t][:], ACT.Abs_reciprocal_sqrt, bias=recips[:, t : t + 1], scale=recips[:, 32 + t : 32 + t + 1])
+
+        backs = {}
+
+        def turn_back(t, blocks, tag):
+            cols = slice(blocks[0] * P, (blocks[-1] + 1) * P)
+            nc.vector.tensor_tensor(root[t][:, cols], res[t][:, cols], damp[t][:, cols], ALU.mult)
+            backs[t, blocks] = turns.tile([P, len(blocks), P], F32, name=f"back{t}_{blocks[0]}", tag=tag)
+            for i, b in enumerate(blocks):
+                nc.tensor.transpose(backs[t, blocks][:, i, :], root[t][:, b * P : (b + 1) * P], ident[:])
+
+        def finish(t, blocks):
+            rows = slice(blocks[0], blocks[-1] + 1)
+            nc.scalar.activation(cost[t][:, rows, :], backs[t, blocks][:], ACT.Square)
+            nc.sync.dma_start(out_rows[:, rows, t * P : (t + 1) * P], cost[t][:, rows, :])
+
+        residual(0)
+        damping(0, False)
+        residual(1)
+        damping(1, False)
+        residual(2)
+        residual(3)
+        turn_back(0, (0, 1), "back")
+        damping(2, True)
+        turn_back(1, (0, 1), "back")
+        damping(3, True)
+        finish(0, (0, 1))
+        turn_back(2, (0, 1), "turn")
+        finish(1, (0, 1))
+        turn_back(3, (0,), "turn")
+        turn_back(3, (1,), "back")
+        finish(2, (0, 1))
+        finish(3, (0,))
+        finish(3, (1,))

from contextlib import ExitStack

import concourse.mybir as mybir
from concourse.masks import make_identity

K, T, S, N, U = 1024, 2048, 512, 256, 256
FLOPS = 2 * K * S * N

F32 = mybir.dt.float32
BF16 = mybir.dt.bfloat16
I32 = mybir.dt.int32
U32 = mybir.dt.uint32
U16 = mybir.dt.uint16
U8 = mybir.dt.uint8
FP8X4 = mybir.dt.float8_e4m3fn_x4
ACT = mybir.ActivationFunctionType
ALU = mybir.AluOpType

P = 128
PACK = 4
PASSES = K // (P * PACK)
BLOCKS = N // P
TILES = S // P
WINDOW = 704
SPARE = WINDOW - U


def tile_picked_yposgr_cost_p_kernel(tc, x_words, x_scales, w1, pose, info, mu, offs, ia, ib, out):
    nc = tc.nc
    with ExitStack() as ctx:
        keep = ctx.enter_context(tc.tile_pool(name="keep", bufs=1))
        ybanks = ctx.enter_context(tc.psum_pool(name="ybanks", bufs=1))
        turns = ctx.enter_context(tc.psum_pool(name="turns", bufs=2))

        ib_sb = keep.tile([P, S // 16], U16, name="ib_sb")
        ia_sb = keep.tile([P, S // 16], U16, name="ia_sb")
        offs_sb = keep.tile([P, S // 16], U16, name="offs_sb")
        poses = keep.tile([P, 2 * BLOCKS * U + SPARE], F32, name="poses")
        start = {("a", 1): 0, ("a", 0): U, ("b", 1): 2 * U, ("b", 0): 3 * U}
        scale_table = keep.tile([P, T], U8, name="scale_table", align_bytes=64)
        word_table = [keep.tile([P, T], I32, name=f"word_table{g}", align_bytes=64) for g in range(PASSES)]
        w_raw = keep.tile([P, PASSES, PACK, N], F32, name="w_raw")
        edge_rows = keep.tile([P, P], F32, name="edge_rows")
        inv_rows = keep.tile([P, P], F32, name="inv_rows")
        ident = keep.tile([P, P], F32, name="ident")

        nc.gpsimd.memset(scale_table[:].bitcast(I32), 0)
        nc.vector.memset(poses[:, 2 * BLOCKS * U :], 0.0)
        nc.vector.memset(inv_rows[:], 0.0)

        nc.sync.dma_start(ib_sb[:], ib)
        nc.sync.dma_start(poses[:, 3 * U : 4 * U], pose[:P, :])
        nc.sync.dma_start(ia_sb[:], ia)
        nc.sync.dma_start(poses[:, 2 * U : 3 * U], pose[P:, :])
        nc.sync.dma_start(w_raw[:].rearrange("p g j n -> p g (j n)"), w1.rearrange("(g p j) n -> p g (j n)", p=P, j=PACK))
        nc.sync.dma_start(offs_sb[:], offs)
        nc.sync.dma_start(word_table[0][:], x_words[0].rearrange("p n t -> p (n t)").bitcast(I32))
        for q in range(4):
            nc.sync.dma_start(scale_table[32 * q : 32 * q + 4 * PASSES, :].bitcast(I32), x_scales[:, 4 * q : 4 * q + 4, :].bitcast(I32))
        nc.sync.dma_start(word_table[1][:], x_words[1].rearrange("p n t -> p (n t)").bitcast(I32))
        nc.scalar.dma_start(edge_rows[:TILES, :], info[0].rearrange("(t c) -> t c", c=P))
        nc.scalar.dma_start(edge_rows[32 : 32 + TILES, :], mu[0].rearrange("(t c) -> t c", c=P))
        nc.scalar.activation(inv_rows[:TILES, :], edge_rows[:TILES, :], ACT.Abs_reciprocal_sqrt)
        make_identity(nc, ident[:])

        for b in range(BLOCKS):
            nc.scalar.activation(poses[:, start["a", b] : start["a", b] + U], poses[:, start["b", b] : start["b", b] + U], ACT.Copy, scale=-1.0)

        nc.scalar.activation(inv_rows[32 : 32 + TILES, :], edge_rows[32 : 32 + TILES, :], ACT.Abs_reciprocal_sqrt)
        nc.scalar.activation(inv_rows[: 32 + TILES, :], inv_rows[: 32 + TILES, :], ACT.Square)
        edge_cols = turns.tile([P, P], F32, name="edge_cols", tag="turn")
        nc.tensor.transpose(edge_cols[:], inv_rows[:], ident[:])
        recips = keep.tile([P, 32 + TILES], F32, name="recips")
        nc.scalar.copy(recips[:], edge_cols[:, : 32 + TILES])

        ends = {}
        for b in range(BLOCKS):
            for name, offsets in (("b", ib_sb), ("a", ia_sb)):
                picked = keep.tile([P, S], F32, name=f"end_{name}{b}")
                nc.vector.tensor_copy(picked[:], poses[:, start[name, b] : start[name, b] + WINDOW].indirect(offsets[:]))
                ends[name, b] = picked

        w_bf = keep.tile([P, PASSES, N, PACK], BF16, name="w_bf", align_bytes=64)
        for g in range(PASSES):
            nc.scalar.copy(w_bf[:, g], w_raw[:, g].rearrange("p j n -> p n j"))
        w_codes = keep.tile([P, PASSES * N], U32, name="w_codes", align_bytes=64)
        w_scales = keep.tile([P, PASSES * N], U8, name="w_scales", align_bytes=64)
        for g in range(PASSES):
            nc.vector.quantize_mx(out=w_codes[:, g * N : (g + 1) * N].bitcast(FP8X4), scales=w_scales[:, g * N : (g + 1) * N], in_=w_bf[:, g].rearrange("p n j -> p (n j)"))

        diff_ps = [turns.tile([P, 2, N], F32, name=f"diff_ps{h}", tag="turn") for h in range(2)]
        for b in range(BLOCKS):
            for t in range(TILES):
                target = diff_ps[t // 2][:, t % 2, b * P : (b + 1) * P]
                nc.tensor.matmul(target, ends["b", b][:, t * P : (t + 1) * P], ident[:], start=True, stop=False, is_transpose=True)
                nc.tensor.matmul(target, ends["a", b][:, t * P : (t + 1) * P], ident[:], start=False, stop=True, is_transpose=True)
        diff = keep.tile([P, TILES, N], F32, name="diff")
        for h in range(2):
            nc.scalar.copy(diff[:, 2 * h : 2 * h + 2, :], diff_ps[h][:])

        x_scale = keep.tile([P, S], U8, name="x_scale", align_bytes=64)
        for h in range(2):
            nc.vector.tensor_copy(x_scale[:, h * 256 : (h + 1) * 256], scale_table[:].indirect(offs_sb[:, h * 16 : (h + 1) * 16]))
        x_codes = [keep.tile([P, S], U32, name=f"x_codes{g}", align_bytes=64) for g in range(PASSES)]
        nc.vector.tensor_copy(x_codes[0][:], word_table[0][:].bitcast(U32).indirect(offs_sb[:]))
        y_ps = [ybanks.tile([P, N], F32, name=f"y_ps{t}") for t in range(TILES)]

        def product(t, g):
            cols = slice(t * P, (t + 1) * P)
            nc.tensor.matmul_mx(
                out=y_ps[t][:],
                lhsT=x_codes[g][:, cols].bitcast(FP8X4),
                lhsT_scale=x_scale[4 * g :, cols],
                rhs=w_codes[:, g * N : (g + 1) * N].bitcast(FP8X4),
                rhs_scale=w_scales[:, g * N : (g + 1) * N],
                start=(g == 0),
                stop=(g == PASSES - 1),
            )

        for t in range(TILES):
            product(t, 0)
        for h in range(2):
            nc.vector.tensor_copy(x_codes[1][:, h * 256 : (h + 1) * 256], word_table[1][:].bitcast(U32).indirect(offs_sb[:, h * 16 : (h + 1) * 16]))
            product(2 * h, 1)
            product(2 * h + 1, 1)

        res = [keep.tile([P, N], F32, name=f"res{t}") for t in range(TILES)]
        sq = [keep.tile([P, N], F32, name=f"sq{t}") for t in range(TILES)]
        damp = [keep.tile([P, N], F32, name=f"damp{t}") for t in range(TILES)]
        root = [keep.tile([P, N], F32, name=f"root{t}") for t in range(TILES)]
        cost = [keep.tile([P, BLOCKS, P], F32, name=f"cost{t}") for t in range(TILES)]
        out_rows = out.rearrange("(b p) s -> p b s", p=P)

        def residual(t):
            nc.vector.tensor_tensor(res[t][:], y_ps[t][:], diff[:, t, :], ALU.subtract)

        def damping(t, on_vector):
            if on_vector:
                nc.vector.tensor_tensor(sq[t][:], res[t][:], res[t][:], ALU.mult)
            else:
                nc.scalar.activation(sq[t][:], res[t][:], ACT.Square)
            nc.scalar.activation(damp[t][:], sq[t][:], ACT.Abs_reciprocal_sqrt, bias=recips[:, t : t + 1], scale=recips[:, 32 + t : 32 + t + 1])

        backs = {}

        def turn_back(t, blocks, tag):
            cols = slice(blocks[0] * P, (blocks[-1] + 1) * P)
            nc.vector.tensor_tensor(root[t][:, cols], res[t][:, cols], damp[t][:, cols], ALU.mult)
            backs[t, blocks] = turns.tile([P, len(blocks), P], F32, name=f"back{t}_{blocks[0]}", tag=tag)
            for i, b in enumerate(blocks):
                nc.tensor.transpose(backs[t, blocks][:, i, :], root[t][:, b * P : (b + 1) * P], ident[:])

        def finish(t, blocks):
            rows = slice(blocks[0], blocks[-1] + 1)
            nc.scalar.activation(cost[t][:, rows, :], backs[t, blocks][:], ACT.Square)
            nc.sync.dma_start(out_rows[:, rows, t * P : (t + 1) * P], cost[t][:, rows, :])

        residual(0)
        damping(0, False)
        residual(1)
        damping(1, False)
        residual(2)
        residual(3)
        turn_back(0, (0, 1), "back")
        damping(2, True)
        turn_back(1, (0, 1), "back")
        damping(3, True)
        finish(0, (0, 1))
        turn_back(2, (0, 1), "turn")
        finish(1, (0, 1))
        turn_back(3, (0,), "turn")
        turn_back(3, (1,), "back")
        finish(2, (0, 1))
        finish(3, (0,))
        finish(3, (1,))
